import numpy as np
import ml_dtypes


def mxq(x, axis, fmt="e4m3"):
    dtype, down = {"e4m3": (ml_dtypes.float8_e4m3fn, 7), "e5m2": (ml_dtypes.float8_e5m2, 14)}[fmt]
    v = np.moveaxis(np.asarray(x, np.float32).astype(ml_dtypes.bfloat16).astype(np.float64), axis, -1)
    blocks = v.reshape(v.shape[:-1] + (-1, 32))
    amax = np.abs(blocks).max(-1, keepdims=True)
    byte = np.maximum(np.where(amax > 0, np.frexp(amax)[1] - 1 + 127, 0) - down, 1)
    scale = np.exp2(byte - 127.0)
    codes = (blocks / scale).astype(np.float32).astype(dtype).astype(np.float64)
    return np.moveaxis((codes * scale).reshape(v.shape), -1, axis)


WIDE = False


def mx_kscale(k):
    if not WIDE:
        return np.ones(k)
    levels = np.array([10, -10, 5, -5, 0])
    if k % 512:
        return np.exp2(np.random.permutation(np.resize(levels, k // 32))).repeat(32)
    a = np.empty((k // 512, 16))
    for p in range(k // 512):
        a[p, :8] = np.random.permutation(np.resize(levels, 8))
        for g in range(8):
            far = levels[np.abs(levels - a[p, g]) >= 10]
            a[p, g + 8] = far[np.random.randint(len(far))]
    return np.exp2(a.ravel()).repeat(32)


def f64(x):
    return np.asarray(x).astype(np.float64)


def striped(idx):
    return np.tile(idx.reshape(-1, 16).T, (8, 1)).astype(np.uint16)


def unstriped(offs):
    return offs[:16].T.reshape(-1).astype(np.int64)


E2M1 = np.array([0.0, 0.5, 1.0, 1.5, 2.0, 3.0, 4.0, 6.0, -0.0, -0.5, -1.0, -1.5, -2.0, -3.0, -4.0, -6.0])


def pack_weight(w, fmt):
    k, n = w.shape
    w = f64(np.asarray(w, np.float32).astype(ml_dtypes.bfloat16)).reshape(k // 32, 32, n)
    amax = np.abs(w).max(1)
    if fmt == "e4m3":
        byte = np.frexp(amax)[1] - 1 + 127 - 7
    else:
        mant, ex = np.frexp(amax / 6.0)
        byte = np.where(mant > 0.5, ex, ex - 1) + 127
    byte = np.clip(np.where(amax > 0, byte, 1), 1, 254)
    scaled = (w * np.exp2(127.0 - byte)[:, None, :]).reshape(k, n).astype(np.float32)
    by_word = np.ascontiguousarray(scaled.reshape(k // 512, 128, 4, n).transpose(0, 1, 3, 2))
    if fmt == "e4m3":
        words = by_word.astype(ml_dtypes.float8_e4m3fn).view(np.uint8)
    else:
        c = by_word.astype(ml_dtypes.float4_e2m1fn).view(np.uint8) & 0xF
        words = (c[..., 0::2] | (c[..., 1::2] << 4)).reshape(k // 512, 128, 2 * n)
    return np.ascontiguousarray(words), np.ascontiguousarray(byte.astype(np.uint8).reshape(k // 512, 16, n))


def unpack_weight(words, scales, fmt):
    g, _, n = scales.shape
    words = np.ascontiguousarray(words).reshape(g, 128, n, -1)
    if fmt == "e4m3":
        vals = words.view(ml_dtypes.float8_e4m3fn).astype(np.float64)
    else:
        nib = np.empty((g, 128, n, 4), np.uint8)
        nib[..., 0::2] = words & 0xF
        nib[..., 1::2] = words >> 4
        vals = E2M1[nib]
    vals = vals * np.repeat(np.exp2(scales.astype(np.float64) - 127.0), 8, axis=1)[..., None]
    return vals.transpose(0, 1, 3, 2).reshape(g * 512, n)


def gelu(v):
    return 0.5 * v * (1.0 + np.tanh(np.sqrt(2.0 / np.pi) * (v + 0.044715 * v**3)))


def bf(x):
    return np.asarray(x, np.float32).astype(ml_dtypes.bfloat16)


def planes(Y):
    n, m = Y.shape
    b = f64(bf(Y)).reshape(n // 32, 32, m)
    amax = np.abs(b).max(1)
    byte = np.clip(np.where(amax > 0, np.frexp(amax)[1] - 1 + 127 - 7, 1), 1, 254)
    codes = (b * np.exp2(127.0 - byte)[:, None, :]).reshape(n, m).astype(np.float32).astype(ml_dtypes.float8_e4m3fn).view(np.uint8)
    words = codes.reshape(n // 512, 128, 4, m).transpose(0, 1, 3, 2)
    return np.ascontiguousarray(words), np.ascontiguousarray(byte.astype(np.uint8).reshape(n // 512, 16, m))


K, T, S, H, P, P2, N = 512, 4096, 1024, 1024, 512, 256, 1024

def setup_inputs():
    n = np.random.standard_normal
    s = mx_kscale(K)[:, None]
    u = mx_kscale(H)[:, None]
    gain = np.exp(0.3 * n((H, 1)))
    amp = np.exp(0.8 * n(N))
    d = {}
    d["tab_words"], d["tab_scales"] = pack_weight(n((K, T)) * s, "e4m3")
    d["offs"] = striped(np.random.permutation(T)[:S])
    d["pos1"] = striped(np.random.permutation(S)[:P])
    d["pos2"] = striped(np.random.permutation(P)[:P2])
    d["w1"] = (n((K, H)) / s * (gain * u).T / K**0.5).astype(np.float32)
    d["wc_words"], d["wc_scales"] = pack_weight(0.52 * n((K, H)) / s / K**0.5, "e2m1")
    d["wt"] = (1.6 * n((H, H)) / u / H**0.5).astype(np.float32)
    d["wo_words"], d["wo_scales"] = pack_weight(n((H, N)) / u * amp / H**0.5, "e4m3")
    d["cvec"] = (0.6 * n(N) * amp).astype(np.float32)
    return d

def reference(tab_words, tab_scales, offs, pos1, pos2, w1, wc_words, wc_scales, wt, wo_words, wo_scales, cvec):
    v = unpack_weight(tab_words, tab_scales, "e4m3")[:, unstriped(offs)]
    wc = unpack_weight(wc_words, wc_scales, "e2m1")
    wo = unpack_weight(wo_words, wo_scales, "e4m3")
    a = mxq(f64(w1), 0, "e4m3").T @ v
    b = wc.T @ v
    h = a * np.cos(b)
    x1 = h[:, unstriped(pos1)]
    p = mxq(f64(wt), 0, "e4m3").T @ mxq(x1, 0, "e4m3")
    x2 = x1 + 0.9 * (x1 * np.tanh(p))
    x3 = x2[:, unstriped(pos2)]
    y = (wo.T @ mxq(x3, 0, "e4m3")) + f64(cvec)[:, None]
    words, scales = planes(y)
    return y, words, scales

@@ -1,0 +1,284 @@
+import math
+from contextlib import ExitStack
+
+import concourse.mybir as mybir
+
+K, T, S, H, P1, P2, N = 512, 4096, 1024, 1024, 512, 256, 1024
+FLOPS = 2 * (2 * K * H * S + H * H * P1 + H * N * P2)
+
+F32 = mybir.dt.float32
+BF16 = mybir.dt.bfloat16
+I32 = mybir.dt.int32
+U32 = mybir.dt.uint32
+U16 = mybir.dt.uint16
+U8 = mybir.dt.uint8
+FP8X4 = mybir.dt.float8_e4m3fn_x4
+FP4X4 = mybir.dt.float4_e2m1fn_x4
+ACT = mybir.ActivationFunctionType
+ALU = mybir.AluOpType
+
+P = 128
+PACK = 4
+G = P * PACK
+STEP = 0.9
+
+
+def tile_list_gloss_handshape_trunk_kernel(
+    tc, tab_words, tab_scales, offs, pos1, pos2, w1, wc_words, wc_scales, wt, wo_words, wo_scales, cvec, out_0, out_1, out_2
+):
+    nc = tc.nc
+    with ExitStack() as ctx:
+        keep = ctx.enter_context(tc.tile_pool(name="keep", bufs=1))
+        stage = ctx.enter_context(tc.tile_pool(name="stage", bufs=2))
+        work = ctx.enter_context(tc.tile_pool(name="work", bufs=3))
+        psum = ctx.enter_context(tc.psum_pool(name="psum", bufs=8))
+
+        def kept(shape, dtype, name):
+            return keep.tile(shape, dtype, name=name, align_bytes=64)
+
+        offs_t = kept([P, S // 16], U16, "offs_t")
+        pos1_t = kept([P, P1 // 16], U16, "pos1_t")
+        pos2_t = kept([P, P2 // 16], U16, "pos2_t")
+        tab_w = keep.tile([P, T], I32, name="tab_w", tag="tab_w", align_bytes=64)
+        tab_s = keep.tile([P, T], U8, name="tab_s", tag="tab_s", align_bytes=64)
+        wc_raw = kept([P, 2 * H], U8, "wc_raw")
+        wc_s_raw = kept([P, H], U8, "wc_s_raw")
+        bias = kept([P, 2, PACK], F32, "bias")
+
+        def load_weight(rows):
+            raw = stage.tile([P, PACK, G], F32, name="raw", align_bytes=64)
+            nc.sync.dma_start(out=raw[:], in_=rows.rearrange("(p j) c -> p j c", j=PACK))
+            return raw
+
+        nc.vector.memset(tab_s[:].bitcast(I32), 0)
+        nc.vector.memset(wc_s_raw[:].bitcast(I32), 0)
+        nc.sync.dma_start(offs_t[:], offs)
+        nc.sync.dma_start(pos1_t[:], pos1)
+        nc.sync.dma_start(pos2_t[:], pos2)
+        w1_raw0 = load_weight(w1[:, 0:G])
+        nc.sync.dma_start(out=tab_w[:], in_=tab_words[0].rearrange("p t i -> p (t i)").bitcast(I32))
+        w1_raw1 = load_weight(w1[:, G : 2 * G])
+        nc.scalar.dma_start(out=wc_raw[:].bitcast(I32), in_=wc_words[0].bitcast(I32))
+        for q in range(4):
+            nc.scalar.dma_start(out=tab_s[32 * q : 32 * q + 4, :].bitcast(I32), in_=tab_scales[0, 4 * q : 4 * q + 4, :].bitcast(I32))
+        for q in range(4):
+            nc.gpsimd.dma_start(out=wc_s_raw[32 * q : 32 * q + 4, :].bitcast(I32), in_=wc_scales[0, 4 * q : 4 * q + 4, :].bitcast(I32))
+        nc.gpsimd.dma_start(out=bias[:], in_=cvec.rearrange("(g p t) -> p g t", g=2, t=PACK))
+
+        def round_weight(engines, raw):
+            grouped = work.tile([P, PACK, P, PACK], BF16, name="w_bf", align_bytes=64)
+            dst = grouped[:].rearrange("p t m j -> p m j t")
+            src = raw[:].rearrange("p j (m t) -> p m j t", t=PACK)
+            share = P // len(engines)
+            for n, engine in enumerate(engines):
+                cols = slice(share * n, share * (n + 1))
+                if engine == "scalar":
+                    nc.scalar.activation(dst[:, cols], src[:, cols], ACT.Copy)
+                else:
+                    nc.vector.tensor_copy(dst[:, cols], src[:, cols])
+            return grouped
+
+        def quantize(name, grouped_flat, width):
+            codes = kept([P, width], U32, name + "_c")
+            scales = kept([P, width], U8, name + "_s")
+            nc.vector.quantize_mx(out=codes[:].bitcast(FP8X4), scales=scales[:], in_=grouped_flat)
+            return codes, scales
+
+        def quantize_weight(name, grouped):
+            return quantize(name, grouped[:].rearrange("p t m j -> p (t m j)"), G)
+
+        v_w = [kept([P, G], U32, f"v_w{h}") for h in range(2)]
+        v_s = [kept([P, G], U8, f"v_s{h}") for h in range(2)]
+
+        def gather_table(dst, window, h):
+            nc.vector.tensor_copy(dst[h][:], window.indirect(offs_t[:, 32 * h : 32 * (h + 1)]))
+
+        w1_bf0 = round_weight(["scalar"], w1_raw0)
+        gather_table(v_s, tab_s[:], 0)
+        wc_w = kept([P, 2 * H], U8, "wc_w")
+        wc_s = kept([P, H], U8, "wc_s")
+        nc.vector.tensor_copy(
+            wc_w[:].rearrange("p (b t m e) -> p b t m e", b=2, t=PACK, e=2),
+            wc_raw[:].rearrange("p (b m t e) -> p b t m e", b=2, t=PACK, e=2),
+        )
+        nc.vector.tensor_copy(
+            wc_s[:].rearrange("p (b t m) -> p b t m", b=2, t=PACK),
+            wc_s_raw[:].rearrange("p (b m t) -> p b t m", b=2, t=PACK),
+        )
+        w1_q = [quantize_weight("w1a", w1_bf0)]
+        gather_table(v_s, tab_s[:], 1)
+        gather_table(v_w, tab_w[:].bitcast(U32), 0)
+        gather_table(v_w, tab_w[:].bitcast(U32), 1)
+
+        x1s = [kept([P, PACK, P1], F32, f"x1s{b}") for b in range(2)]
+        x1_q = []
+        wt_raw = {}
+        wt_bf = {}
+        wt_q = {}
+        turns, shape, picked, whole, frac, cosine = {}, {}, {}, {}, {}, {}
+
+        def first_products(i):
+            b, t = divmod(i, PACK)
+            turns[i] = work.tile([P, S], F32, name="turns")
+            shape[i] = work.tile([P, S], F32, name="shape", bufs=4)
+            for h in range(2):
+                bank = psum.tile([P, G], F32, name="bank")
+                nc.tensor.matmul_mx(
+                    out=bank[:], lhsT=wc_w[:, 2 * P * i : 2 * P * (i + 1)].bitcast(FP4X4), lhsT_scale=wc_s[:, P * i : P * (i + 1)],
+                    rhs=v_w[h][:].bitcast(FP8X4), rhs_scale=v_s[h][:], start=True, stop=True,
+                )
+                nc.scalar.activation(turns[i][:, G * h : G * (h + 1)], bank[:], ACT.Copy, bias=0.25, scale=1.0 / (2.0 * math.pi))
+            codes, scales = w1_q[b]
+            for h in range(2):
+                bank = psum.tile([P, G], F32, name="bank")
+                nc.tensor.matmul_mx(
+                    out=bank[:], lhsT=codes[:, P * t : P * (t + 1)].bitcast(FP8X4), lhsT_scale=scales[:, P * t : P * (t + 1)],
+                    rhs=v_w[h][:].bitcast(FP8X4), rhs_scale=v_s[h][:], start=True, stop=True,
+                )
+                nc.scalar.activation(shape[i][:, G * h : G * (h + 1)], bank[:], ACT.Copy, scale=STEP)
+
+        def pick_phase(i):
+            picked[i] = work.tile([P, P1], F32, name="picked")
+            nc.vector.tensor_copy(picked[i][:], turns[i][:].indirect(pos1_t[:]))
+
+        def whole_turns(i):
+            whole[i] = work.tile([P, P1], I32, name="whole")
+            nc.vector.tensor_copy(whole[i][:], picked[i][:])
+
+        def cos_of(i):
+            frac[i] = work.tile([P, P1], F32, name="frac")
+            cosine[i] = work.tile([P, P1], F32, name="cosine")
+            nc.vector.tensor_tensor(frac[i][:], picked[i][:], whole[i][:], ALU.subtract)
+            nc.scalar.activation(cosine[i][:], frac[i][:], ACT.Sin, scale=2.0 * math.pi)
+
+        def pick_shape(i):
+            b, t = divmod(i, PACK)
+            nc.vector.tensor_tensor(x1s[b][:, t, :], shape[i][:].indirect(pos1_t[:]), cosine[i][:], ALU.mult)
+
+        def interleave(name, src, width, scale, engines):
+            grouped = kept([P, width, PACK], BF16, name + "_bf")
+            share = width // len(engines)
+            for n, engine in enumerate(engines):
+                cols = slice(share * n, share * (n + 1))
+                dst_ap = grouped[:, cols, :].rearrange("p (c i) t -> p c t i", i=4)
+                src_ap = src[:, :, cols].rearrange("p t (c i) -> p c t i", i=4)
+                if engine == "scalar":
+                    nc.scalar.activation(dst_ap, src_ap, ACT.Copy, scale=scale)
+                else:
+                    nc.vector.tensor_scalar(dst_ap, src_ap, scale, None, ALU.mult)
+            return grouped[:].rearrange("p c t -> p (c t)")
+
+        def wt_load(a, b):
+            wt_raw[a, b] = load_weight(wt[G * a : G * (a + 1), G * b : G * (b + 1)])
+
+        def wt_round(a, b):
+            wt_bf[a, b] = round_weight(["scalar", "scalar"], wt_raw[a, b])
+
+        def wt_quantize(a, b):
+            wt_q[a, b] = quantize_weight(f"wt{a}{b}", wt_bf[a, b])
+
+        x1_bf = {}
+        for s in range(8 + 2):
+            if s == 1:
+                w1_bf1 = round_weight(["vector"], w1_raw1)
+            if s == 2:
+                w1_q.append(quantize_weight("w1b", w1_bf1))
+            if s < 8:
+                first_products(s)
+                pick_phase(s)
+            if 1 <= s < 9:
+                cos_of(s - 1)
+            if s < 8:
+                whole_turns(s)
+            if s >= 2:
+                pick_shape(s - 2)
+            if s in (2, 4):
+                wt_load(s // 2 - 1, 0)
+                wt_round(s // 2 - 1, 0)
+            if s in (3, 5):
+                wt_quantize(s // 2 - 1, 0)
+            if s == 5:
+                x1_bf[0] = interleave("x1a", x1s[0], P1, 1.0 / STEP, ["scalar"])
+            if s == 6:
+                x1_q.append(quantize("x1a", x1_bf[0], P1))
+        x1_bf[1] = interleave("x1b", x1s[1], P1, 1.0 / STEP, ["scalar", "vector"])
+        x1_q.append(quantize("x1b", x1_bf[1], P1))
+        wt_load(0, 1)
+        wt_load(1, 1)
+
+        wo_raw = keep.tile([P, 2, N], I32, name="wo_raw", tag="tab_w", align_bytes=64)
+        nc.sync.dma_start(out=wo_raw[:], in_=wo_words.rearrange("a p c i -> p a (c i)").bitcast(I32))
+        wo_s_raw = keep.tile([P, N], U8, name="wo_s_raw", tag="tab_s", align_bytes=64)
+        nc.gpsimd.memset(wo_s_raw[:].bitcast(I32), 0)
+        for q in range(4):
+            nc.sync.dma_start(out=wo_s_raw[32 * q : 32 * q + 8, :].bitcast(I32), in_=wo_scales[:, 4 * q : 4 * q + 4, :].bitcast(I32))
+        wo_w = kept([P, 2, N], I32, "wo_w")
+        wo_s = kept([P, N], U8, "wo_s")
+
+        x3 = [kept([P, PACK, P2], F32, f"x3{b}") for b in range(2)]
+        x3_q = []
+        x2 = {}
+        x3_bf = {}
+        for s in range(8 + 1):
+            if s < 8:
+                b, t = divmod(s, PACK)
+                bank = psum.tile([P, P1], F32, name="bank")
+                for a in range(2):
+                    codes, scales = wt_q[a, b]
+                    nc.tensor.matmul_mx(
+                        out=bank[:], lhsT=codes[:, P * t : P * (t + 1)].bitcast(FP8X4), lhsT_scale=scales[:, P * t : P * (t + 1)],
+                        rhs=x1_q[a][0][:].bitcast(FP8X4), rhs_scale=x1_q[a][1][:], start=(a == 0), stop=(a == 1),
+                    )
+                th = work.tile([P, P1], F32, name="th")
+                nc.scalar.activation(th[:], bank[:], ACT.Tanh)
+                x2[s] = work.tile([P, P1], F32, name="x2")
+                nc.vector.scalar_tensor_tensor(x2[s][:], th[:], 1.0 / STEP, x1s[b][:, t, :], ALU.add, ALU.mult)
+            if s >= 1:
+                b, t = divmod(s - 1, PACK)
+                nc.vector.tensor_copy(x3[b][:, t, :], x2[s - 1][:].indirect(pos2_t[:]))
+            if s in (0, 1):
+                wt_round(s, 1)
+            if s in (2, 3):
+                wt_quantize(s - 2, 1)
+            if s == 4:
+                x3_bf[0] = interleave("x3a", x3[0], P2, 1.0, ["scalar"])
+            if s == 5:
+                x3_q.append(quantize("x3a", x3_bf[0], P2))
+            if s == 6:
+                nc.vector.tensor_copy(
+                    wo_w[:].rearrange("p a (g t m) -> p (a g) m t", g=2, t=PACK),
+                    wo_raw[:].rearrange("p a (g m t) -> p (a g) m t", g=2, t=PACK),
+                )
+                nc.vector.tensor_copy(
+                    wo_s[:].rearrange("p (g t m) -> p g t m", g=2, t=PACK),
+                    wo_s_raw[:].rearrange("p (g m t) -> p g t m", g=2, t=PACK),
+                )
+        x3_bf[1] = interleave("x3b", x3[1], P2, 1.0, ["scalar", "vector"])
+        x3_q.append(quantize("x3b", x3_bf[1], P2))
+
+        y_s = kept([P, 2, P2], U8, "y_s")
+        for g in range(2):
+            y = kept([P, PACK, P2], F32, f"y{g}")
+            for t in range(PACK):
+                cols = slice(G * g + P * t, G * g + P * (t + 1))
+                bank = psum.tile([P, G], F32, name="bank")
+                for a in range(2):
+                    nc.tensor.matmul_mx(
+                        out=bank[:, 0:P2], lhsT=wo_w[:, a, cols].bitcast(FP8X4), lhsT_scale=wo_s[4 * a :, cols],
+                        rhs=x3_q[a][0][:].bitcast(FP8X4), rhs_scale=x3_q[a][1][:], start=(a == 0), stop=(a == 1),
+                    )
+                if t % 2 == 0:
+                    nc.scalar.activation(y[:, t, :], bank[:, 0:P2], ACT.Identity, bias=bias[:, g, t : t + 1])
+                else:
+                    nc.vector.tensor_scalar(y[:, t, :], bank[:, 0:P2], bias[:, g, t : t + 1], None, ALU.add)
+            nc.sync.dma_start(out=out_0[G * g : G * (g + 1), :].rearrange("(p t) j -> p t j", t=PACK), in_=y[:])
+            y_bf = kept([P, P2, PACK], BF16, f"y_bf{g}")
+            nc.vector.tensor_copy(y_bf[:].rearrange("p (c i) t -> p c t i", i=4), y[:].rearrange("p t (c i) -> p c t i", i=4))
+            y_c = kept([P, P2], I32, f"y_c{g}")
+            nc.vector.quantize_mx(out=y_c[:].bitcast(FP8X4), scales=y_s[:, g, :], in_=y_bf[:].rearrange("p c t -> p (c t)"))
+            nc.sync.dma_start(out=out_1[g].rearrange("p m t -> p (m t)").bitcast(I32), in_=y_c[:])
+        for q in range(4):
+            eng = nc.sync if q % 2 == 0 else nc.scalar
+            eng.dma_start(
+                out=out_2[:, 4 * q : 4 * q + 4, :].rearrange("g r m -> r g m").bitcast(I32), in_=y_s[32 * q : 32 * q + 4, :, :].bitcast(I32)
+            )

@@ -21,6 +21,8 @@ P = 128
 PACK = 4
 G = P * PACK
 STEP = 0.9
+ROW0 = P - 16
+WO_ROW0 = ROW0 - 32
 
 
 def tile_list_gloss_handshape_trunk_kernel(
@@ -39,34 +41,35 @@ def tile_list_gloss_handshape_trunk_kernel(
         offs_t = kept([P, S // 16], U16, "offs_t")
         pos1_t = kept([P, P1 // 16], U16, "pos1_t")
         pos2_t = kept([P, P2 // 16], U16, "pos2_t")
-        tab_w = keep.tile([P, T], I32, name="tab_w", tag="tab_w", align_bytes=64)
-        tab_s = keep.tile([P, T], U8, name="tab_s", tag="tab_s", align_bytes=64)
+        tab_s = kept([P, T], U8, "tab_s")
         wc_raw = kept([P, 2 * H], U8, "wc_raw")
-        wc_s_raw = kept([P, H], U8, "wc_s_raw")
+        tab_w = keep.tile([P, T], I32, name="tab_w", tag="tab_w", align_bytes=64)
+        w_s_raw = kept([P, H], U8, "w_s_raw")
+        rows = kept([P, H + S], U8, "rows")
+        first_s = kept([P, H + S], U8, "first_s")
         bias = kept([P, 2, PACK], F32, "bias")
 
-        def load_weight(rows):
-            raw = stage.tile([P, PACK, G], F32, name="raw", align_bytes=64)
-            nc.sync.dma_start(out=raw[:], in_=rows.rearrange("(p j) c -> p j c", j=PACK))
+        def load_weight(part):
+            raw = stage.tile([P, PACK, G], F32, name="raw", tag="raw", align_bytes=64)
+            nc.sync.dma_start(out=raw[:], in_=part.rearrange("(p j) c -> p j c", j=PACK))
             return raw
 
-        nc.vector.memset(tab_s[:].bitcast(I32), 0)
-        nc.vector.memset(wc_s_raw[:].bitcast(I32), 0)
+        nc.vector.memset(tab_s[0:ROW0, :].bitcast(I32), 0)
+        nc.gpsimd.memset(w_s_raw[0:WO_ROW0, :].bitcast(I32), 0)
+        nc.sync.dma_start(out=w_s_raw[ROW0:P, :].bitcast(I32), in_=wc_scales[0].bitcast(I32))
+        nc.sync.dma_start(out=w_s_raw[WO_ROW0:ROW0, :].bitcast(I32), in_=wo_scales.rearrange("a q c -> (a q) c").bitcast(I32))
+        nc.sync.dma_start(out=tab_s[ROW0:P, :].bitcast(I32), in_=tab_scales[0].bitcast(I32))
         nc.sync.dma_start(offs_t[:], offs)
+        nc.sync.dma_start(out=wc_raw[:].bitcast(I32), in_=wc_words[0].bitcast(I32))
         nc.sync.dma_start(pos1_t[:], pos1)
         nc.sync.dma_start(pos2_t[:], pos2)
-        w1_raw0 = load_weight(w1[:, 0:G])
         nc.sync.dma_start(out=tab_w[:], in_=tab_words[0].rearrange("p t i -> p (t i)").bitcast(I32))
-        w1_raw1 = load_weight(w1[:, G : 2 * G])
-        nc.scalar.dma_start(out=wc_raw[:].bitcast(I32), in_=wc_words[0].bitcast(I32))
-        for q in range(4):
-            nc.scalar.dma_start(out=tab_s[32 * q : 32 * q + 4, :].bitcast(I32), in_=tab_scales[0, 4 * q : 4 * q + 4, :].bitcast(I32))
-        for q in range(4):
-            nc.gpsimd.dma_start(out=wc_s_raw[32 * q : 32 * q + 4, :].bitcast(I32), in_=wc_scales[0, 4 * q : 4 * q + 4, :].bitcast(I32))
+        w1_raw0 = load_weight(w1[:, 0:G])
+        nc.gpsimd.memset(first_s[:].bitcast(I32), 0)
         nc.gpsimd.dma_start(out=bias[:], in_=cvec.rearrange("(g p t) -> p g t", g=2, t=PACK))
 
-        def round_weight(engines, raw):
-            grouped = work.tile([P, PACK, P, PACK], BF16, name="w_bf", align_bytes=64)
+        def round_weight(engines, raw, tag="w_bf", bufs=2):
+            grouped = work.tile([P, PACK, P, PACK], BF16, name="w_bf", tag=tag, bufs=bufs, align_bytes=64)
             dst = grouped[:].rearrange("p t m j -> p m j t")
             src = raw[:].rearrange("p j (m t) -> p m j t", t=PACK)
             share = P // len(engines)
@@ -87,28 +90,30 @@ def tile_list_gloss_handshape_trunk_kernel(
         def quantize_weight(name, grouped):
             return quantize(name, grouped[:].rearrange("p t m j -> p (t m j)"), G)
 
-        v_w = [kept([P, G], U32, f"v_w{h}") for h in range(2)]
-        v_s = [kept([P, G], U8, f"v_s{h}") for h in range(2)]
+        v_w = [keep.tile([P, G], U32, name=f"v_w{h}", tag=f"v_w{h}", align_bytes=64) for h in range(2)]
+        v_s = stage.tile([P, S], U8, name="v_s", tag="raw", align_bytes=64)
 
         def gather_table(dst, window, h):
             nc.vector.tensor_copy(dst[h][:], window.indirect(offs_t[:, 32 * h : 32 * (h + 1)]))
 
-        w1_bf0 = round_weight(["scalar"], w1_raw0)
-        gather_table(v_s, tab_s[:], 0)
         wc_w = kept([P, 2 * H], U8, "wc_w")
-        wc_s = kept([P, H], U8, "wc_s")
         nc.vector.tensor_copy(
-            wc_w[:].rearrange("p (b t m e) -> p b t m e", b=2, t=PACK, e=2),
-            wc_raw[:].rearrange("p (b m t e) -> p b t m e", b=2, t=PACK, e=2),
+            rows[:, 0:H].rearrange("p (b t m) -> p b t m", b=2, t=PACK),
+            w_s_raw[:].rearrange("p (b m t) -> p b t m", b=2, t=PACK),
         )
+        nc.vector.tensor_copy(v_s[:], tab_s[:].indirect(offs_t[:]))
+        nc.vector.tensor_copy(rows[:, H : H + S].bitcast(I32), v_s[:].bitcast(I32))
+        for q in range(4):
+            nc.sync.dma_start(
+                out=first_s[32 * q : 32 * q + 4, :].bitcast(I32), in_=rows[ROW0 + 4 * q : ROW0 + 4 * q + 4, :].bitcast(I32)
+            )
         nc.vector.tensor_copy(
-            wc_s[:].rearrange("p (b t m) -> p b t m", b=2, t=PACK),
-            wc_s_raw[:].rearrange("p (b m t) -> p b t m", b=2, t=PACK),
+            wc_w[:].bitcast(U16).rearrange("p (b t m) -> p b m t", b=2, t=PACK),
+            wc_raw[:].bitcast(U16).rearrange("p (b m t) -> p b m t", b=2, t=PACK),
         )
-        w1_q = [quantize_weight("w1a", w1_bf0)]
-        gather_table(v_s, tab_s[:], 1)
         gather_table(v_w, tab_w[:].bitcast(U32), 0)
         gather_table(v_w, tab_w[:].bitcast(U32), 1)
+        w1_q = []
 
         x1s = [kept([P, PACK, P1], F32, f"x1s{b}") for b in range(2)]
         x1_q = []
@@ -117,23 +122,25 @@ def tile_list_gloss_handshape_trunk_kernel(
         wt_q = {}
         turns, shape, picked, whole, frac, cosine = {}, {}, {}, {}, {}, {}
 
-        def first_products(i):
-            b, t = divmod(i, PACK)
+        def phase_products(i):
             turns[i] = work.tile([P, S], F32, name="turns")
-            shape[i] = work.tile([P, S], F32, name="shape", bufs=4)
             for h in range(2):
                 bank = psum.tile([P, G], F32, name="bank")
                 nc.tensor.matmul_mx(
-                    out=bank[:], lhsT=wc_w[:, 2 * P * i : 2 * P * (i + 1)].bitcast(FP4X4), lhsT_scale=wc_s[:, P * i : P * (i + 1)],
-                    rhs=v_w[h][:].bitcast(FP8X4), rhs_scale=v_s[h][:], start=True, stop=True,
+                    out=bank[:], lhsT=wc_w[:, 2 * P * i : 2 * P * (i + 1)].bitcast(FP4X4), lhsT_scale=first_s[:, P * i : P * (i + 1)],
+                    rhs=v_w[h][:].bitcast(FP8X4), rhs_scale=first_s[:, H + G * h : H + G * (h + 1)], start=True, stop=True,
                 )
                 nc.scalar.activation(turns[i][:, G * h : G * (h + 1)], bank[:], ACT.Copy, bias=0.25, scale=1.0 / (2.0 * math.pi))
+
+        def shape_products(i):
+            b, t = divmod(i, PACK)
+            shape[i] = work.tile([P, S], F32, name="shape", tag="shape", bufs=4, align_bytes=64)
             codes, scales = w1_q[b]
             for h in range(2):
                 bank = psum.tile([P, G], F32, name="bank")
                 nc.tensor.matmul_mx(
                     out=bank[:], lhsT=codes[:, P * t : P * (t + 1)].bitcast(FP8X4), lhsT_scale=scales[:, P * t : P * (t + 1)],
-                    rhs=v_w[h][:].bitcast(FP8X4), rhs_scale=v_s[h][:], start=True, stop=True,
+                    rhs=v_w[h][:].bitcast(FP8X4), rhs_scale=first_s[:, H + G * h : H + G * (h + 1)], start=True, stop=True,
                 )
                 nc.scalar.activation(shape[i][:, G * h : G * (h + 1)], bank[:], ACT.Copy, scale=STEP)
 
@@ -142,13 +149,15 @@ def tile_list_gloss_handshape_trunk_kernel(
             nc.vector.tensor_copy(picked[i][:], turns[i][:].indirect(pos1_t[:]))
 
         def whole_turns(i):
-            whole[i] = work.tile([P, P1], I32, name="whole")
+            whole[i] = work.tile([P, P1], I32, name="whole", bufs=1)
             nc.vector.tensor_copy(whole[i][:], picked[i][:])
 
         def cos_of(i):
-            frac[i] = work.tile([P, P1], F32, name="frac")
-            cosine[i] = work.tile([P, P1], F32, name="cosine")
+            frac[i] = work.tile([P, P1], F32, name="frac", bufs=2)
             nc.vector.tensor_tensor(frac[i][:], picked[i][:], whole[i][:], ALU.subtract)
+
+        def sine(i):
+            cosine[i] = work.tile([P, P1], F32, name="cosine")
             nc.scalar.activation(cosine[i][:], frac[i][:], ACT.Sin, scale=2.0 * math.pi)
 
         def pick_shape(i):
@@ -172,34 +181,43 @@ def tile_list_gloss_handshape_trunk_kernel(
             wt_raw[a, b] = load_weight(wt[G * a : G * (a + 1), G * b : G * (b + 1)])
 
         def wt_round(a, b):
-            wt_bf[a, b] = round_weight(["scalar", "scalar"], wt_raw[a, b])
+            wt_bf[a, b] = round_weight(["scalar", "scalar"], wt_raw[a, b], *(("w_bf", 2) if b == 0 else ("shape", 4)))
 
         def wt_quantize(a, b):
             wt_q[a, b] = quantize_weight(f"wt{a}{b}", wt_bf[a, b])
 
         x1_bf = {}
-        for s in range(8 + 2):
-            if s == 1:
-                w1_bf1 = round_weight(["vector"], w1_raw1)
-            if s == 2:
-                w1_q.append(quantize_weight("w1b", w1_bf1))
+        for s in range(8 + 3):
             if s < 8:
-                first_products(s)
+                phase_products(s)
                 pick_phase(s)
+            if s == 0:
+                w1_bf0 = round_weight(["scalar", "scalar"], w1_raw0)
+                w1_raw1 = load_weight(w1[:, G : 2 * G])
+            if s == 1:
+                w1_q.append(quantize_weight("w1a", w1_bf0))
+            if 1 <= s < 9:
+                shape_products(s - 1)
+            if s >= 3:
+                sine(s - 3)
             if 1 <= s < 9:
                 cos_of(s - 1)
+            if s >= 3:
+                pick_shape(s - 3)
             if s < 8:
                 whole_turns(s)
-            if s >= 2:
-                pick_shape(s - 2)
-            if s in (2, 4):
+            if s == 2:
+                w1_bf1 = round_weight(["vector"], w1_raw1)
+            if s == 3:
+                w1_q.append(quantize_weight("w1b", w1_bf1))
+            if s in (3, 5):
                 wt_load(s // 2 - 1, 0)
                 wt_round(s // 2 - 1, 0)
-            if s in (3, 5):
-                wt_quantize(s // 2 - 1, 0)
-            if s == 5:
+            if s in (4, 6):
+                wt_quantize(s // 2 - 2, 0)
+            if s == 7:
                 x1_bf[0] = interleave("x1a", x1s[0], P1, 1.0 / STEP, ["scalar"])
-            if s == 6:
+            if s == 8:
                 x1_q.append(quantize("x1a", x1_bf[0], P1))
         x1_bf[1] = interleave("x1b", x1s[1], P1, 1.0 / STEP, ["scalar", "vector"])
         x1_q.append(quantize("x1b", x1_bf[1], P1))
@@ -208,12 +226,24 @@ def tile_list_gloss_handshape_trunk_kernel(
 
         wo_raw = keep.tile([P, 2, N], I32, name="wo_raw", tag="tab_w", align_bytes=64)
         nc.sync.dma_start(out=wo_raw[:], in_=wo_words.rearrange("a p c i -> p a (c i)").bitcast(I32))
-        wo_s_raw = keep.tile([P, N], U8, name="wo_s_raw", tag="tab_s", align_bytes=64)
-        nc.gpsimd.memset(wo_s_raw[:].bitcast(I32), 0)
-        for q in range(4):
-            nc.sync.dma_start(out=wo_s_raw[32 * q : 32 * q + 8, :].bitcast(I32), in_=wo_scales[:, 4 * q : 4 * q + 4, :].bitcast(I32))
-        wo_w = kept([P, 2, N], I32, "wo_w")
-        wo_s = kept([P, N], U8, "wo_s")
+        wo_s = keep.tile([P, N], U8, name="wo_s", tag="v_w0", align_bytes=64)
+        nc.gpsimd.memset(wo_s[:].bitcast(I32), 0)
+        for a in range(2):
+            for q in range(4):
+                src = WO_ROW0 + 16 * a + 4 * q
+                nc.sync.dma_start(
+                    out=wo_s[32 * q + 4 * a : 32 * q + 4 * a + 4, :].bitcast(I32), in_=rows[src : src + 4, 0:N].bitcast(I32)
+                )
+        wt_round(0, 1)
+        wt_round(1, 1)
+        wo_w = []
+        for a in range(2):
+            dealt = work.tile([P, N], I32, name="wo_w", tag="shape", bufs=4, align_bytes=64)
+            nc.vector.tensor_copy(
+                dealt[:].rearrange("p (g t m) -> p g m t", g=2, t=PACK),
+                wo_raw[:, a, :].rearrange("p (g m t) -> p g m t", g=2, t=PACK),
+            )
+            wo_w.append(dealt)
 
         x3 = [kept([P, PACK, P2], F32, f"x3{b}") for b in range(2)]
         x3_q = []
@@ -236,23 +266,24 @@ def tile_list_gloss_handshape_trunk_kernel(
             if s >= 1:
                 b, t = divmod(s - 1, PACK)
                 nc.vector.tensor_copy(x3[b][:, t, :], x2[s - 1][:].indirect(pos2_t[:]))
-            if s in (0, 1):
-                wt_round(s, 1)
             if s in (2, 3):
                 wt_quantize(s - 2, 1)
             if s == 4:
                 x3_bf[0] = interleave("x3a", x3[0], P2, 1.0, ["scalar"])
             if s == 5:
                 x3_q.append(quantize("x3a", x3_bf[0], P2))
-            if s == 6:
-                nc.vector.tensor_copy(
-                    wo_w[:].rearrange("p a (g t m) -> p (a g) m t", g=2, t=PACK),
-                    wo_raw[:].rearrange("p a (g m t) -> p (a g) m t", g=2, t=PACK),
-                )
-                nc.vector.tensor_copy(
-                    wo_s[:].rearrange("p (g t m) -> p g t m", g=2, t=PACK),
-                    wo_s_raw[:].rearrange("p (g m t) -> p g t m", g=2, t=PACK),
-                )
+        y_banks = []
+
+        def last_product(i, a):
+            cols = slice(P * i, P * (i + 1))
+            nc.tensor.matmul_mx(
+                out=y_banks[i][:, 0:P2], lhsT=wo_w[a][:, cols].bitcast(FP8X4), lhsT_scale=wo_s[4 * a :, cols],
+                rhs=x3_q[a][0][:].bitcast(FP8X4), rhs_scale=x3_q[a][1][:], start=(a == 0), stop=(a == 1),
+            )
+
+        for i in range(8):
+            y_banks.append(psum.tile([P, G], F32, name="bank"))
+            last_product(i, 0)
         x3_bf[1] = interleave("x3b", x3[1], P2, 1.0, ["scalar", "vector"])
         x3_q.append(quantize("x3b", x3_bf[1], P2))
 
@@ -260,22 +291,16 @@ def tile_list_gloss_handshape_trunk_kernel(
         for g in range(2):
             y = kept([P, PACK, P2], F32, f"y{g}")
             for t in range(PACK):
-                cols = slice(G * g + P * t, G * g + P * (t + 1))
-                bank = psum.tile([P, G], F32, name="bank")
-                for a in range(2):
-                    nc.tensor.matmul_mx(
-                        out=bank[:, 0:P2], lhsT=wo_w[:, a, cols].bitcast(FP8X4), lhsT_scale=wo_s[4 * a :, cols],
-                        rhs=x3_q[a][0][:].bitcast(FP8X4), rhs_scale=x3_q[a][1][:], start=(a == 0), stop=(a == 1),
-                    )
-                if t % 2 == 0:
+                bank = y_banks[PACK * g + t]
+                last_product(PACK * g + t, 1)
+                if t % 2 == 0 or g == 1:
                     nc.scalar.activation(y[:, t, :], bank[:, 0:P2], ACT.Identity, bias=bias[:, g, t : t + 1])
                 else:
                     nc.vector.tensor_scalar(y[:, t, :], bank[:, 0:P2], bias[:, g, t : t + 1], None, ALU.add)
             nc.sync.dma_start(out=out_0[G * g : G * (g + 1), :].rearrange("(p t) j -> p t j", t=PACK), in_=y[:])
-            y_bf = kept([P, P2, PACK], BF16, f"y_bf{g}")
-            nc.vector.tensor_copy(y_bf[:].rearrange("p (c i) t -> p c t i", i=4), y[:].rearrange("p t (c i) -> p c t i", i=4))
+            y_bf = interleave(f"y{g}", y, P2, 1.0, ["vector"] if g == 0 else ["scalar", "vector"])
             y_c = kept([P, P2], I32, f"y_c{g}")
-            nc.vector.quantize_mx(out=y_c[:].bitcast(FP8X4), scales=y_s[:, g, :], in_=y_bf[:].rearrange("p c t -> p (c t)"))
+            nc.vector.quantize_mx(out=y_c[:].bitcast(FP8X4), scales=y_s[:, g, :], in_=y_bf)
             nc.sync.dma_start(out=out_1[g].rearrange("p m t -> p (m t)").bitcast(I32), in_=y_c[:])
         for q in range(4):
             eng = nc.sync if q % 2 == 0 else nc.scalar

@@ -144,25 +144,36 @@ def tile_list_gloss_handshape_trunk_kernel(
                 )
                 nc.scalar.activation(shape[i][:, G * h : G * (h + 1)], bank[:], ACT.Copy, scale=STEP)
 
+        def x1s_rows(i):
+            return x1s[i // PACK][:, i % PACK, :]
+
+        first_picked = kept([P, 2, P1], F32, "first_picked")
+
         def pick_phase(i):
-            picked[i] = work.tile([P, P1], F32, name="picked")
-            nc.vector.tensor_copy(picked[i][:], turns[i][:].indirect(pos1_t[:]))
+            picked[i] = first_picked[:, i, :] if i < 2 else x1s_rows(i - 2)
+            nc.vector.tensor_copy(picked[i], turns[i][:].indirect(pos1_t[:]))
 
         def whole_turns(i):
-            whole[i] = work.tile([P, P1], I32, name="whole", bufs=1)
-            nc.vector.tensor_copy(whole[i][:], picked[i][:])
+            whole[i] = work.tile([P, P1], I32, name="whole", bufs=2)
+            nc.gpsimd.tensor_scalar(whole[i][:], picked[i], 1.0, 0.0, ALU.mult, ALU.add)
 
         def cos_of(i):
             frac[i] = work.tile([P, P1], F32, name="frac", bufs=2)
-            nc.vector.tensor_tensor(frac[i][:], picked[i][:], whole[i][:], ALU.subtract)
+            nc.vector.tensor_tensor(frac[i][:], picked[i], whole[i][:], ALU.subtract)
 
         def sine(i):
-            cosine[i] = work.tile([P, P1], F32, name="cosine")
+            cosine[i] = work.tile([P, P1], F32, name="cosine", bufs=4)
             nc.scalar.activation(cosine[i][:], frac[i][:], ACT.Sin, scale=2.0 * math.pi)
 
+        gained = {}
+
         def pick_shape(i):
-            b, t = divmod(i, PACK)
-            nc.vector.tensor_tensor(x1s[b][:, t, :], shape[i][:].indirect(pos1_t[:]), cosine[i][:], ALU.mult)
+            gained[i] = work.tile([P, P1], F32, name="gained", bufs=4)
+            nc.vector.tensor_copy(gained[i][:], shape[i][:].indirect(pos1_t[:]))
+
+        def multiply(i):
+            engine = nc.gpsimd if i < 6 else nc.vector
+            engine.tensor_tensor(x1s_rows(i), gained[i][:], cosine[i][:], ALU.mult)
 
         def interleave(name, src, width, scale, engines):
             grouped = kept([P, width, PACK], BF16, name + "_bf")
@@ -181,7 +192,7 @@ def tile_list_gloss_handshape_trunk_kernel(
             wt_raw[a, b] = load_weight(wt[G * a : G * (a + 1), G * b : G * (b + 1)])
 
         def wt_round(a, b):
-            wt_bf[a, b] = round_weight(["scalar", "scalar"], wt_raw[a, b], *(("w_bf", 2) if b == 0 else ("shape", 4)))
+            wt_bf[a, b] = round_weight(["vector"] if (a, b) == (0, 0) else ["scalar", "scalar"], wt_raw[a, b], *(("w_bf", 2) if b == 0 else ("shape", 4)))
 
         def wt_quantize(a, b):
             wt_q[a, b] = quantize_weight(f"wt{a}{b}", wt_bf[a, b])
@@ -191,6 +202,7 @@ def tile_list_gloss_handshape_trunk_kernel(
             if s < 8:
                 phase_products(s)
                 pick_phase(s)
+                whole_turns(s)
             if s == 0:
                 w1_bf0 = round_weight(["scalar", "scalar"], w1_raw0)
                 w1_raw1 = load_weight(w1[:, G : 2 * G])
@@ -198,14 +210,13 @@ def tile_list_gloss_handshape_trunk_kernel(
                 w1_q.append(quantize_weight("w1a", w1_bf0))
             if 1 <= s < 9:
                 shape_products(s - 1)
+                pick_shape(s - 1)
             if s >= 3:
                 sine(s - 3)
             if 1 <= s < 9:
                 cos_of(s - 1)
             if s >= 3:
-                pick_shape(s - 3)
-            if s < 8:
-                whole_turns(s)
+                multiply(s - 3)
             if s == 2:
                 w1_bf1 = round_weight(["vector"], w1_raw1)
             if s == 3:

import math
from contextlib import ExitStack

import concourse.mybir as mybir

K, T, S, H, P1, P2, N = 512, 4096, 1024, 1024, 512, 256, 1024
FLOPS = 2 * (2 * K * H * S + H * H * P1 + H * N * P2)

F32 = mybir.dt.float32
BF16 = mybir.dt.bfloat16
I32 = mybir.dt.int32
U32 = mybir.dt.uint32
U16 = mybir.dt.uint16
U8 = mybir.dt.uint8
FP8X4 = mybir.dt.float8_e4m3fn_x4
FP4X4 = mybir.dt.float4_e2m1fn_x4
ACT = mybir.ActivationFunctionType
ALU = mybir.AluOpType

P = 128
PACK = 4
G = P * PACK
STEP = 0.9
ROW0 = P - 16
WO_ROW0 = ROW0 - 32


def tile_list_gloss_handshape_trunk_kernel(
    tc, tab_words, tab_scales, offs, pos1, pos2, w1, wc_words, wc_scales, wt, wo_words, wo_scales, cvec, out_0, out_1, out_2
):
    nc = tc.nc
    with ExitStack() as ctx:
        keep = ctx.enter_context(tc.tile_pool(name="keep", bufs=1))
        stage = ctx.enter_context(tc.tile_pool(name="stage", bufs=2))
        work = ctx.enter_context(tc.tile_pool(name="work", bufs=3))
        psum = ctx.enter_context(tc.psum_pool(name="psum", bufs=8))

        def kept(shape, dtype, name):
            return keep.tile(shape, dtype, name=name, align_bytes=64)

        offs_t = kept([P, S // 16], U16, "offs_t")
        pos1_t = kept([P, P1 // 16], U16, "pos1_t")
        pos2_t = kept([P, P2 // 16], U16, "pos2_t")
        tab_s = kept([P, T], U8, "tab_s")
        wc_raw = kept([P, 2 * H], U8, "wc_raw")
        tab_w = keep.tile([P, T], I32, name="tab_w", tag="tab_w", align_bytes=64)
        w_s_raw = kept([P, H], U8, "w_s_raw")
        rows = kept([P, H + S], U8, "rows")
        first_s = kept([P, H + S], U8, "first_s")
        bias = kept([P, 2, PACK], F32, "bias")

        def load_weight(part):
            raw = stage.tile([P, PACK, G], F32, name="raw", tag="raw", align_bytes=64)
            nc.sync.dma_start(out=raw[:], in_=part.rearrange("(p j) c -> p j c", j=PACK))
            return raw

        nc.vector.memset(tab_s[0:ROW0, :].bitcast(I32), 0)
        nc.gpsimd.memset(w_s_raw[0:WO_ROW0, :].bitcast(I32), 0)
        nc.sync.dma_start(out=w_s_raw[ROW0:P, :].bitcast(I32), in_=wc_scales[0].bitcast(I32))
        nc.sync.dma_start(out=w_s_raw[WO_ROW0:ROW0, :].bitcast(I32), in_=wo_scales.rearrange("a q c -> (a q) c").bitcast(I32))
        nc.sync.dma_start(out=tab_s[ROW0:P, :].bitcast(I32), in_=tab_scales[0].bitcast(I32))
        nc.sync.dma_start(offs_t[:], offs)
        nc.sync.dma_start(out=wc_raw[:].bitcast(I32), in_=wc_words[0].bitcast(I32))
        nc.sync.dma_start(pos1_t[:], pos1)
        nc.sync.dma_start(pos2_t[:], pos2)
        nc.sync.dma_start(out=tab_w[:], in_=tab_words[0].rearrange("p t i -> p (t i)").bitcast(I32))
        w1_raw0 = load_weight(w1[:, 0:G])
        nc.gpsimd.memset(first_s[:].bitcast(I32), 0)
        nc.gpsimd.dma_start(out=bias[:], in_=cvec.rearrange("(g p t) -> p g t", g=2, t=PACK))

        def round_weight(engines, raw, tag="w_bf", bufs=2):
            grouped = work.tile([P, PACK, P, PACK], BF16, name="w_bf", tag=tag, bufs=bufs, align_bytes=64)
            dst = grouped[:].rearrange("p t m j -> p m j t")
            src = raw[:].rearrange("p j (m t) -> p m j t", t=PACK)
            share = P // len(engines)
            for n, engine in enumerate(engines):
                cols = slice(share * n, share * (n + 1))
                if engine == "scalar":
                    nc.scalar.activation(dst[:, cols], src[:, cols], ACT.Copy)
                else:
                    nc.vector.tensor_copy(dst[:, cols], src[:, cols])
            return grouped

        def quantize(name, grouped_flat, width):
            codes = kept([P, width], U32, name + "_c")
            scales = kept([P, width], U8, name + "_s")
            nc.vector.quantize_mx(out=codes[:].bitcast(FP8X4), scales=scales[:], in_=grouped_flat)
            return codes, scales

        def quantize_weight(name, grouped):
            return quantize(name, grouped[:].rearrange("p t m j -> p (t m j)"), G)

        v_w = [keep.tile([P, G], U32, name=f"v_w{h}", tag=f"v_w{h}", align_bytes=64) for h in range(2)]
        v_s = stage.tile([P, S], U8, name="v_s", tag="raw", align_bytes=64)

        def gather_table(dst, window, h):
            nc.vector.tensor_copy(dst[h][:], window.indirect(offs_t[:, 32 * h : 32 * (h + 1)]))

        wc_w = kept([P, 2 * H], U8, "wc_w")
        nc.vector.tensor_copy(
            rows[:, 0:H].rearrange("p (b t m) -> p b t m", b=2, t=PACK),
            w_s_raw[:].rearrange("p (b m t) -> p b t m", b=2, t=PACK),
        )
        nc.vector.tensor_copy(v_s[:], tab_s[:].indirect(offs_t[:]))
        nc.vector.tensor_copy(rows[:, H : H + S].bitcast(I32), v_s[:].bitcast(I32))
        for q in range(4):
            nc.sync.dma_start(
                out=first_s[32 * q : 32 * q + 4, :].bitcast(I32), in_=rows[ROW0 + 4 * q : ROW0 + 4 * q + 4, :].bitcast(I32)
            )
        nc.vector.tensor_copy(
            wc_w[:].bitcast(U16).rearrange("p (b t m) -> p b m t", b=2, t=PACK),
            wc_raw[:].bitcast(U16).rearrange("p (b m t) -> p b m t", b=2, t=PACK),
        )
        gather_table(v_w, tab_w[:].bitcast(U32), 0)
        gather_table(v_w, tab_w[:].bitcast(U32), 1)
        w1_q = []

        x1s = [kept([P, PACK, P1], F32, f"x1s{b}") for b in range(2)]
        x1_q = []
        wt_raw = {}
        wt_bf = {}
        wt_q = {}
        turns, shape, picked, whole, frac, cosine = {}, {}, {}, {}, {}, {}

        def phase_products(i):
            turns[i] = work.tile([P, S], F32, name="turns")
            for h in range(2):
                bank = psum.tile([P, G], F32, name="bank")
                nc.tensor.matmul_mx(
                    out=bank[:], lhsT=wc_w[:, 2 * P * i : 2 * P * (i + 1)].bitcast(FP4X4), lhsT_scale=first_s[:, P * i : P * (i + 1)],
                    rhs=v_w[h][:].bitcast(FP8X4), rhs_scale=first_s[:, H + G * h : H + G * (h + 1)], start=True, stop=True,
                )
                nc.scalar.activation(turns[i][:, G * h : G * (h + 1)], bank[:], ACT.Copy, bias=0.25, scale=1.0 / (2.0 * math.pi))

        def shape_products(i):
            b, t = divmod(i, PACK)
            shape[i] = work.tile([P, S], F32, name="shape", tag="shape", bufs=4, align_bytes=64)
            codes, scales = w1_q[b]
            for h in range(2):
                bank = psum.tile([P, G], F32, name="bank")
                nc.tensor.matmul_mx(
                    out=bank[:], lhsT=codes[:, P * t : P * (t + 1)].bitcast(FP8X4), lhsT_scale=scales[:, P * t : P * (t + 1)],
                    rhs=v_w[h][:].bitcast(FP8X4), rhs_scale=first_s[:, H + G * h : H + G * (h + 1)], start=True, stop=True,
                )
                nc.scalar.activation(shape[i][:, G * h : G * (h + 1)], bank[:], ACT.Copy, scale=STEP)

        def x1s_rows(i):
            return x1s[i // PACK][:, i % PACK, :]

        first_picked = kept([P, 2, P1], F32, "first_picked")

        def pick_phase(i):
            picked[i] = first_picked[:, i, :] if i < 2 else x1s_rows(i - 2)
            nc.vector.tensor_copy(picked[i], turns[i][:].indirect(pos1_t[:]))

        def whole_turns(i):
            whole[i] = work.tile([P, P1], I32, name="whole", bufs=2)
            nc.gpsimd.tensor_scalar(whole[i][:], picked[i], 1.0, 0.0, ALU.mult, ALU.add)

        def cos_of(i):
            frac[i] = work.tile([P, P1], F32, name="frac", bufs=2)
            nc.vector.tensor_tensor(frac[i][:], picked[i], whole[i][:], ALU.subtract)

        def sine(i):
            cosine[i] = work.tile([P, P1], F32, name="cosine", bufs=4)
            nc.scalar.activation(cosine[i][:], frac[i][:], ACT.Sin, scale=2.0 * math.pi)

        gained = {}

        def pick_shape(i):
            gained[i] = work.tile([P, P1], F32, name="gained", bufs=4)
            nc.vector.tensor_copy(gained[i][:], shape[i][:].indirect(pos1_t[:]))

        def multiply(i):
            engine = nc.gpsimd if i < 6 else nc.vector
            engine.tensor_tensor(x1s_rows(i), gained[i][:], cosine[i][:], ALU.mult)

        def interleave(name, src, width, scale, engines):
            grouped = kept([P, width, PACK], BF16, name + "_bf")
            share = width // len(engines)
            for n, engine in enumerate(engines):
                cols = slice(share * n, share * (n + 1))
                dst_ap = grouped[:, cols, :].rearrange("p (c i) t -> p c t i", i=4)
                src_ap = src[:, :, cols].rearrange("p t (c i) -> p c t i", i=4)
                if engine == "scalar":
                    nc.scalar.activation(dst_ap, src_ap, ACT.Copy, scale=scale)
                else:
                    nc.vector.tensor_scalar(dst_ap, src_ap, scale, None, ALU.mult)
            return grouped[:].rearrange("p c t -> p (c t)")

        def wt_load(a, b):
            wt_raw[a, b] = load_weight(wt[G * a : G * (a + 1), G * b : G * (b + 1)])

        def wt_round(a, b):
            wt_bf[a, b] = round_weight(["vector"] if (a, b) == (0, 0) else ["scalar", "scalar"], wt_raw[a, b], *(("w_bf", 2) if b == 0 else ("shape", 4)))

        def wt_quantize(a, b):
            wt_q[a, b] = quantize_weight(f"wt{a}{b}", wt_bf[a, b])

        x1_bf = {}
        for s in range(8 + 3):
            if s < 8:
                phase_products(s)
                pick_phase(s)
                whole_turns(s)
            if s == 0:
                w1_bf0 = round_weight(["scalar", "scalar"], w1_raw0)
                w1_raw1 = load_weight(w1[:, G : 2 * G])
            if s == 1:
                w1_q.append(quantize_weight("w1a", w1_bf0))
            if 1 <= s < 9:
                shape_products(s - 1)
                pick_shape(s - 1)
            if s >= 3:
                sine(s - 3)
            if 1 <= s < 9:
                cos_of(s - 1)
            if s >= 3:
                multiply(s - 3)
            if s == 2:
                w1_bf1 = round_weight(["vector"], w1_raw1)
            if s == 3:
                w1_q.append(quantize_weight("w1b", w1_bf1))
            if s in (3, 5):
                wt_load(s // 2 - 1, 0)
                wt_round(s // 2 - 1, 0)
            if s in (4, 6):
                wt_quantize(s // 2 - 2, 0)
            if s == 7:
                x1_bf[0] = interleave("x1a", x1s[0], P1, 1.0 / STEP, ["scalar"])
            if s == 8:
                x1_q.append(quantize("x1a", x1_bf[0], P1))
        x1_bf[1] = interleave("x1b", x1s[1], P1, 1.0 / STEP, ["scalar", "vector"])
        x1_q.append(quantize("x1b", x1_bf[1], P1))
        wt_load(0, 1)
        wt_load(1, 1)

        wo_raw = keep.tile([P, 2, N], I32, name="wo_raw", tag="tab_w", align_bytes=64)
        nc.sync.dma_start(out=wo_raw[:], in_=wo_words.rearrange("a p c i -> p a (c i)").bitcast(I32))
        wo_s = keep.tile([P, N], U8, name="wo_s", tag="v_w0", align_bytes=64)
        nc.gpsimd.memset(wo_s[:].bitcast(I32), 0)
        for a in range(2):
            for q in range(4):
                src = WO_ROW0 + 16 * a + 4 * q
                nc.sync.dma_start(
                    out=wo_s[32 * q + 4 * a : 32 * q + 4 * a + 4, :].bitcast(I32), in_=rows[src : src + 4, 0:N].bitcast(I32)
                )
        wt_round(0, 1)
        wt_round(1, 1)
        wo_w = []
        for a in range(2):
            dealt = work.tile([P, N], I32, name="wo_w", tag="shape", bufs=4, align_bytes=64)
            nc.vector.tensor_copy(
                dealt[:].rearrange("p (g t m) -> p g m t", g=2, t=PACK),
                wo_raw[:, a, :].rearrange("p (g m t) -> p g m t", g=2, t=PACK),
            )
            wo_w.append(dealt)

        x3 = [kept([P, PACK, P2], F32, f"x3{b}") for b in range(2)]
        x3_q = []
        x2 = {}
        x3_bf = {}
        for s in range(8 + 1):
            if s < 8:
                b, t = divmod(s, PACK)
                bank = psum.tile([P, P1], F32, name="bank")
                for a in range(2):
                    codes, scales = wt_q[a, b]
                    nc.tensor.matmul_mx(
                        out=bank[:], lhsT=codes[:, P * t : P * (t + 1)].bitcast(FP8X4), lhsT_scale=scales[:, P * t : P * (t + 1)],
                        rhs=x1_q[a][0][:].bitcast(FP8X4), rhs_scale=x1_q[a][1][:], start=(a == 0), stop=(a == 1),
                    )
                th = work.tile([P, P1], F32, name="th")
                nc.scalar.activation(th[:], bank[:], ACT.Tanh)
                x2[s] = work.tile([P, P1], F32, name="x2")
                nc.vector.scalar_tensor_tensor(x2[s][:], th[:], 1.0 / STEP, x1s[b][:, t, :], ALU.add, ALU.mult)
            if s >= 1:
                b, t = divmod(s - 1, PACK)
                nc.vector.tensor_copy(x3[b][:, t, :], x2[s - 1][:].indirect(pos2_t[:]))
            if s in (2, 3):
                wt_quantize(s - 2, 1)
            if s == 4:
                x3_bf[0] = interleave("x3a", x3[0], P2, 1.0, ["scalar"])
            if s == 5:
                x3_q.append(quantize("x3a", x3_bf[0], P2))
        y_banks = []

        def last_product(i, a):
            cols = slice(P * i, P * (i + 1))
            nc.tensor.matmul_mx(
                out=y_banks[i][:, 0:P2], lhsT=wo_w[a][:, cols].bitcast(FP8X4), lhsT_scale=wo_s[4 * a :, cols],
                rhs=x3_q[a][0][:].bitcast(FP8X4), rhs_scale=x3_q[a][1][:], start=(a == 0), stop=(a == 1),
            )

        for i in range(8):
            y_banks.append(psum.tile([P, G], F32, name="bank"))
            last_product(i, 0)
        x3_bf[1] = interleave("x3b", x3[1], P2, 1.0, ["scalar", "vector"])
        x3_q.append(quantize("x3b", x3_bf[1], P2))

        y_s = kept([P, 2, P2], U8, "y_s")
        for g in range(2):
            y = kept([P, PACK, P2], F32, f"y{g}")
            for t in range(PACK):
                bank = y_banks[PACK * g + t]
                last_product(PACK * g + t, 1)
                if t % 2 == 0 or g == 1:
                    nc.scalar.activation(y[:, t, :], bank[:, 0:P2], ACT.Identity, bias=bias[:, g, t : t + 1])
                else:
                    nc.vector.tensor_scalar(y[:, t, :], bank[:, 0:P2], bias[:, g, t : t + 1], None, ALU.add)
            nc.sync.dma_start(out=out_0[G * g : G * (g + 1), :].rearrange("(p t) j -> p t j", t=PACK), in_=y[:])
            y_bf = interleave(f"y{g}", y, P2, 1.0, ["vector"] if g == 0 else ["scalar", "vector"])
            y_c = kept([P, P2], I32, f"y_c{g}")
            nc.vector.quantize_mx(out=y_c[:].bitcast(FP8X4), scales=y_s[:, g, :], in_=y_bf)
            nc.sync.dma_start(out=out_1[g].rearrange("p m t -> p (m t)").bitcast(I32), in_=y_c[:])
        for q in range(4):
            eng = nc.sync if q % 2 == 0 else nc.scalar
            eng.dma_start(
                out=out_2[:, 4 * q : 4 * q + 4, :].rearrange("g r m -> r g m").bitcast(I32), in_=y_s[32 * q : 32 * q + 4, :, :].bitcast(I32)
            )
